import numpy as np
import ml_dtypes


def mxq(x, axis, fmt="e4m3"):
    dtype, down = {"e4m3": (ml_dtypes.float8_e4m3fn, 7), "e5m2": (ml_dtypes.float8_e5m2, 14)}[fmt]
    v = np.moveaxis(np.asarray(x, np.float32).astype(ml_dtypes.bfloat16).astype(np.float64), axis, -1)
    blocks = v.reshape(v.shape[:-1] + (-1, 32))
    amax = np.abs(blocks).max(-1, keepdims=True)
    byte = np.maximum(np.where(amax > 0, np.frexp(amax)[1] - 1 + 127, 0) - down, 1)
    scale = np.exp2(byte - 127.0)
    codes = (blocks / scale).astype(np.float32).astype(dtype).astype(np.float64)
    return np.moveaxis((codes * scale).reshape(v.shape), -1, axis)


WIDE = False


def mx_kscale(k):
    if not WIDE:
        return np.ones(k)
    levels = np.array([10, -10, 5, -5, 0])
    if k % 512:
        return np.exp2(np.random.permutation(np.resize(levels, k // 32))).repeat(32)
    a = np.empty((k // 512, 16))
    for p in range(k // 512):
        a[p, :8] = np.random.permutation(np.resize(levels, 8))
        for g in range(8):
            far = levels[np.abs(levels - a[p, g]) >= 10]
            a[p, g + 8] = far[np.random.randint(len(far))]
    return np.exp2(a.ravel()).repeat(32)


BF16 = ml_dtypes.bfloat16


def bf(x):
    return np.asarray(x, np.float32).astype(BF16)


def f64(x):
    return np.asarray(x).astype(np.float64)


E2M1 = np.array([0.0, 0.5, 1.0, 1.5, 2.0, 3.0, 4.0, 6.0, -0.0, -0.5, -1.0, -1.5, -2.0, -3.0, -4.0, -6.0])


def pack_weight(w, fmt):
    k, n = w.shape
    w = f64(bf(w)).reshape(k // 32, 32, n)
    amax = np.abs(w).max(1)
    if fmt == "e4m3":
        byte = np.frexp(amax)[1] - 1 + 127 - 7
    else:
        mant, ex = np.frexp(amax / 6.0)
        byte = np.where(mant > 0.5, ex, ex - 1) + 127
    byte = np.clip(np.where(amax > 0, byte, 1), 1, 254)
    scaled = (w * np.exp2(127.0 - byte)[:, None, :]).reshape(k, n).astype(np.float32)
    by_word = np.ascontiguousarray(scaled.reshape(k // 512, 128, 4, n).transpose(0, 1, 3, 2))
    if fmt == "e4m3":
        words = by_word.astype(ml_dtypes.float8_e4m3fn).view(np.uint8)
    else:
        c = by_word.astype(ml_dtypes.float4_e2m1fn).view(np.uint8) & 0xF
        words = c[..., 0::2] | (c[..., 1::2] << 4)
    return np.ascontiguousarray(words), np.ascontiguousarray(byte.astype(np.uint8).reshape(k // 512, 16, n))


def unpack_weight(words, scales, fmt):
    g, p, n, _ = words.shape
    if fmt == "e4m3":
        vals = np.ascontiguousarray(words).view(ml_dtypes.float8_e4m3fn).astype(np.float64)
    else:
        nib = np.empty((g, p, n, 4), np.uint8)
        nib[..., 0::2] = words & 0xF
        nib[..., 1::2] = words >> 4
        vals = E2M1[nib]
    vals = vals * np.repeat(np.exp2(scales.astype(np.float64) - 127.0), 8, axis=1)[..., None]
    return vals.transpose(0, 1, 3, 2).reshape(g * 512, n)
def pack4(w):
    words, scales = pack_weight(w, "e2m1")
    return words.reshape(words.shape[0], 128, -1), scales


def unpack4(words, scales):
    return unpack_weight(words.reshape(words.shape[0], 128, -1, 2), scales, "e2m1")


def planes(Y):
    n, m = Y.shape
    b = f64(bf(Y)).reshape(n // 32, 32, m)
    amax = np.abs(b).max(1)
    byte = np.clip(np.where(amax > 0, np.frexp(amax)[1] - 1 + 127 - 7, 1), 1, 254)
    codes = (b * np.exp2(127.0 - byte)[:, None, :]).reshape(n, m).astype(np.float32).astype(ml_dtypes.float8_e4m3fn).view(np.uint8)
    words = codes.reshape(n // 512, 128, 4, m).transpose(0, 1, 3, 2)
    return np.ascontiguousarray(words), np.ascontiguousarray(byte.astype(np.uint8).reshape(n // 512, 16, m))


B, T, C, N, TAPS, D = 4, 256, 1024, 2048, 3, 2
PAST = (TAPS - 1) * D

def setup_inputs():
    s = mx_kscale(C)
    x = np.random.randn(B, PAST + T, C)
    taps = 0.6 * np.random.randn(TAPS, C)
    spread = np.exp(0.8 * np.random.randn(N))
    wv = np.random.randn(C, N) / np.sqrt(C) * spread
    wg = np.random.randn(C, N) / np.sqrt(C)
    wv_words, wv_scales = pack4(wv / s[:, None])
    wg_words, wg_scales = pack4(wg / s[:, None])
    return {
        "x": bf(x),
        "taps": bf(taps * s),
        "wv_words": wv_words, "wv_scales": wv_scales,
        "wg_words": wg_words, "wg_scales": wg_scales,
        "bv": bf(0.3 * np.random.randn(N) * spread),
        "bg": bf(0.5 * np.random.randn(N)),
    }

def reference(x, taps, wv_words, wv_scales, wg_words, wg_scales, bv, bg):
    x, taps, bv, bg = f64(x), f64(taps), f64(bv), f64(bg)
    wv = unpack4(wv_words, wv_scales)
    wg = unpack4(wg_words, wg_scales)
    h = taps[0] * x[:, PAST:PAST + T]
    for j in range(1, TAPS):
        h = h + taps[j] * x[:, PAST - j * D:PAST - j * D + T]
    hq = mxq(h.reshape(B * T, C), 1, "e4m3")
    v = (hq @ wv) + bv
    g = (hq @ wg) + bg
    y = (v * (1.0 / (1.0 + np.exp(-g)))).reshape(B, T, N)
    Y = y.reshape(B * T, N).T
    words, scales = planes(Y)
    return y, words, scales

@@ -1,0 +1,426 @@
+from contextlib import ExitStack
+
+import concourse.mybir as mybir
+from concourse.masks import make_identity
+
+F32 = mybir.dt.float32
+BF16 = mybir.dt.bfloat16
+I32 = mybir.dt.int32
+U32 = mybir.dt.uint32
+U8 = mybir.dt.uint8
+FP8X4 = mybir.dt.float8_e4m3fn_x4
+FP4X4 = mybir.dt.float4_e2m1fn_x4
+ACT = mybir.ActivationFunctionType
+ALU = mybir.AluOpType
+
+B, T, C, N, PAST = 4, 256, 1024, 2048, 4
+FLOPS = 2 * 2 * B * T * C * N
+P = 128
+TOK = 512
+NY = 4
+KB = 1
+EARLY = 4
+HALF = False
+NO = 3
+SKEW = 1
+NA = 3
+NF = 2
+NB = 3
+UNITS = [(h, j) for h in range(2) for j in range(4)]
+PLAN = [
+    ("setup",), ("load_x", 0, 0), ("cast_taps",), ("turn_x", 0, 0, 0), ("turn_x", 0, 0, 1), ("lag0", 0, 0, 0),
+    ("load_scales",), ("load_x", 0, 1), ("load_words", 0, 1), ("lag0", 0, 0, 1), ("load_words", 1, 2),
+    ("turn_x", 0, 1, 0), ("clear_planes",), ("turn_x", 0, 1, 1), ("perm_scales",), ("load_x", 1, 0), ("load_brow",),
+    ("lag1", 0, 0, 0), ("lag0", 0, 0, 2), ("lag0", 0, 0, 3), ("lag0", 0, 1, 0), ("load_bias",), ("lag0", 0, 1, 1),
+    ("load_words", 2, 3), ("lag1", 0, 0, 1), ("far", 0, 0, 0), ("lag1", 0, 0, 2), ("place_scales", 0),
+    ("turn_hist",), ("lag0", 0, 1, 2), ("copy_hist",), ("lag0", 0, 1, 3), ("lag1", 0, 0, 3), ("far", 0, 0, 1),
+    ("lag1", 0, 1, 0), ("perm", 4), ("lag1", 0, 1, 1), ("far", 0, 0, 2), ("make_edge",), ("far", 0, 0, 3),
+    ("place_scales", 2), ("far_edge", 0, 0), ("lag1", 0, 1, 2), ("cast_brow",), ("turn_x", 1, 0, 0), ("turn_brow",),
+    ("far_edge", 0, 1), ("turn_x", 1, 0, 1), ("far", 0, 1, 0), ("copy_brow",), ("place_scales", 1),
+    ("lag1", 0, 1, 3), ("perm", 5), ("far", 0, 1, 1), ("far", 0, 1, 2), ("add_far", "V", 0, 0, 512),
+    ("load_x", 1, 1), ("far", 0, 1, 3), ("lag0", 1, 0, 0), ("perm", 6), ("quant_h", 0, 0), ("far_edge", 1, 0),
+    ("passes", 0, 0, 0, 0, 512, 0, 1), ("passes", 0, 0, 1, 0, 512, 0, 1), ("add_far", "V", 1, 0, 512),
+    ("far", 1, 0, 0), ("passes", 0, 1, 0, 0, 512, 0, 1), ("perm", 7), ("lag0", 1, 0, 1), ("turn_x", 1, 1, 0),
+    ("turn_x", 1, 1, 1), ("quant_h", 0, 1), ("lag0", 1, 0, 2), ("lag0", 1, 0, 3), ("cast_bias",), ("far", 1, 0, 1),
+    ("lag0", 1, 1, 0), ("passes", 0, 1, 1, 0, 512, 0, 1), ("place_scales", 3), ("passes", 0, 0, 0, 0, 512, 1, 2),
+    ("lag1", 1, 0, 0), ("far", 1, 0, 2), ("passes", 0, 0, 1, 0, 512, 1, 2), ("passes", 0, 1, 0, 0, 512, 1, 2),
+    ("load_words", 3, 4), ("lag1", 1, 0, 1), ("passes", 0, 1, 1, 0, 512, 1, 2), ("lag1", 1, 0, 2), ("block", 1),
+    ("block", 2), ("perm", 8), ("lag0", 1, 1, 1), ("block", 3), ("far", 1, 0, 3), ("lag0", 1, 1, 2),
+    ("lag1", 1, 0, 3), ("lag1", 1, 1, 0), ("block", 4), ("lag0", 1, 1, 3), ("perm", 9), ("block", 5),
+    ("turn", 0, 0), ("turn", 0, 1), ("far_edge", 1, 1), ("block", 6), ("add_far", "V", 2, 0, 512), ("far", 1, 1, 0),
+    ("drain", "S", 0, 0), ("drain", "S", 0, 1), ("block", 7), ("far", 1, 1, 1), ("perm", 10), ("turn", 0, 2),
+    ("turn", 0, 3), ("block", 8), ("lag1", 1, 1, 1), ("far", 1, 1, 2), ("drain", "S", 0, 2), ("block", 9),
+    ("far", 1, 1, 3), ("perm", 11), ("block", 10), ("drain", "S", 0, 3), ("perm", 12), ("lag1", 1, 1, 2),
+    ("block", 11), ("lag1", 1, 1, 3), ("cast", "S", 0, 0, 512), ("turn", 1, 0), ("perm", 13), ("quant_h", 1, 0),
+    ("block", 12), ("turn", 1, 1), ("perm", 14), ("back", 0, 0), ("back", 0, 1), ("block", 13), ("evac", "S", 0, 0),
+    ("turn", 1, 2), ("evac", "S", 0, 1), ("drain", "S", 1, 0), ("turn", 1, 3), ("store_y", 0, 0, 2),
+    ("drain", "S", 1, 1), ("drain", "S", 1, 2), ("drain", "S", 1, 3), ("perm", 15), ("add_far", "V", 3, 0, 512),
+    ("block", 14), ("store_y", 0, 2, 4), ("turn", 2, 0), ("turn", 2, 1), ("turn", 2, 2), ("store_y", 1, 0, 2),
+    ("quant_h", 1, 1), ("turn", 2, 3), ("block", 15), ("drain", "S", 2, 0), ("block", 16), ("drain", "S", 2, 1),
+    ("inter_y", "V", 1, 0, 512), ("block", 17), ("quant_y", 0, 0, 512), ("drain", "S", 2, 2), ("turn", 3, 0),
+    ("quant_y", 1, 0, 512), ("turn", 3, 1), ("store_y", 1, 2, 4), ("drain", "S", 2, 3), ("turn", 3, 2),
+    ("turn", 3, 3), ("block", 18), ("store_codes", 0, 0, 512), ("drain", "S", 3, 0), ("store_y", 2, 0, 2),
+    ("drain", "S", 3, 1), ("block", 19), ("drain", "V", 3, 2), ("drain", "S", 3, 3), ("block", 20),
+    ("inter_y", "V", 2, 0, 512), ("quant_y", 2, 0, 512), ("block", 21), ("turn", 4, 0), ("store_y", 2, 2, 4),
+    ("drain", "V", 4, 0), ("inter_y", "S", 3, 0, 512), ("turn", 4, 1), ("turn", 4, 2), ("turn", 4, 3),
+    ("block", 22), ("block", 23), ("drain", "V", 4, 1), ("drain", "S", 4, 2), ("block", 24),
+    ("store_codes", 1, 0, 512), ("store_y", 3, 0, 2), ("drain", "S", 4, 3), ("cast", "V", 4, 0, 512),
+    ("store_codes", 2, 0, 512), ("block", 25), ("store_y", 3, 2, 4), ("turn", 5, 0), ("quant_y", 3, 0, 512),
+    ("turn", 5, 1), ("back", 4, 0), ("back", 4, 1), ("store_y", 4, 0, 2), ("block", 26), ("drain", "S", 5, 0),
+    ("drain", "S", 5, 1), ("evac", "S", 4, 0), ("inter_y", "V", 5, 0, 512), ("store_y", 4, 2, 4),
+    ("evac", "S", 4, 1), ("store_codes", 3, 0, 512), ("quant_y", 4, 0, 512), ("block", 27), ("turn", 5, 2),
+    ("turn", 5, 3), ("store_y", 5, 0, 2), ("block", 28), ("store_scales", 0, 0), ("turn", 6, 0),
+    ("drain", "S", 5, 2), ("turn", 6, 1), ("turn", 6, 2), ("store_scales", 0, 1), ("quant_y", 5, 0, 512),
+    ("drain", "S", 5, 3), ("inter_y", "V", 6, 0, 512), ("store_scales", 0, 2), ("turn", 6, 3), ("block", 29),
+    ("drain", "S", 6, 0), ("quant_y", 6, 0, 512), ("drain", "S", 6, 1), ("drain", "V", 6, 2), ("drain", "S", 6, 3),
+    ("block", 30), ("store_scales", 0, 3), ("block", 31), ("store_codes", 4, 0, 512), ("store_codes", 5, 0, 512),
+    ("gate", 7, 3), ("value", 7, 3, 0, 128), ("value", 7, 3, 128, 256), ("turn", 7, 0, 0, 3), ("turn", 7, 0, 3, 4),
+    ("drain", "S", 7, 0), ("value", 7, 3, 256, 384), ("turn", 7, 1, 0, 3), ("store_y", 5, 2, 4),
+    ("store_y", 6, 0, 2), ("store_scales", 1, 0, 0, 3), ("turn", 7, 1, 3, 4), ("store_y", 6, 2, 4),
+    ("store_scales", 1, 1, 0, 3), ("turn", 7, 2, 0, 3), ("store_codes", 6, 0, 512), ("store_scales", 1, 2, 0, 3),
+    ("drain", "S", 7, 1), ("store_scales", 1, 3, 0, 3), ("value", 7, 3, 384, 512), ("inter_y", "V", 7, 0, 256),
+    ("store_y", 7, 0, 1), ("turn", 7, 2, 3, 4), ("quant_y", 7, 0, 256), ("drain", "S", 7, 2),
+    ("inter_y", "V", 7, 256, 512), ("store_codes", 7, 0, 256), ("store_y", 7, 1, 2), ("turn", 7, 3, 0, 3),
+    ("store_y", 7, 2, 3), ("quant_y", 7, 256, 512), ("store_scales", 1, 0, 3, 4), ("store_scales", 1, 1, 3, 4),
+    ("store_scales", 1, 2, 3, 4), ("turn", 7, 3, 3, 4), ("drain", "S", 7, 3), ("store_y", 7, 3, 4),
+    ("store_scales", 1, 3, 3, 4), ("store_codes", 7, 256, 512),
+]
+
+
+def tile_lag_mix_gated_channels_g4_kernel(
+    tc, x, taps, wv_words, wv_scales, wg_words, wg_scales, bv, bg, out_0, out_1, out_2
+):
+    nc = tc.nc
+    w_words = (wg_words, wv_words)
+    w_scales = (wg_scales, wv_scales)
+    y_rows = out_0.rearrange("b u n -> (b u) n")
+
+    with ExitStack() as ctx:
+        keep = ctx.enter_context(tc.tile_pool(name="keep", bufs=1))
+        psum = ctx.enter_context(tc.psum_pool(name="psum", bufs=1))
+        ctx.enter_context(tc.manual_schedule())
+
+        banks = [psum.tile([P, 512], F32, name="bank%d" % i) for i in range(8)]
+        ident = keep.tile([P, P], F32, name="ident")
+        warm = keep.tile([P, 1], F32, name="warm")
+        warm_out = keep.tile([P, 1], F32, name="warm_out")
+        taps_raw = keep.tile([P, 6, 4], BF16, name="taps_raw")
+        taps_f = keep.tile([P, 3, 8], F32, name="taps_f")
+        bias_raw = [keep.tile([P, 4, 4], BF16, name="bias_raw%d" % m) for m in range(2)]
+        bias_f = keep.tile([P, 2, 16], F32, name="bias_f")
+        x_sb = [[keep.tile([P, 2, 2, 512], BF16, name="x%d%d" % (h, g)) for g in range(2)] for h in range(2)]
+        hist = keep.tile([P, C], BF16, name="hist")
+        hist_w = keep.tile([P, 4, 16], F32, name="hist_w")
+        edge1 = keep.tile([P, 8, 16], F32, name="edge1")
+        edge = keep.tile([P, 8, 16], F32, name="edge")
+        w_raw = keep.tile([P, 4, 4096], U8, name="w_raw", align_bytes=64)
+        brow = keep.tile([P, P], BF16, name="brow")
+        brow_f = keep.tile([P, P], F32, name="brow_f")
+        bias_n = keep.tile([P, 2, 16], F32, name="bias_n")
+        cbs = [keep.tile([P, 2, 4, 256], BF16, name="cb%d" % i) for i in range(2)]
+        s_raw = keep.tile([P, N], U8, name="s_raw")
+        s_mid = keep.tile([P, N], U8, name="s_mid")
+        w_perm = keep.tile([P, max(16 - 4 * KB, 1), 4, 256], U8, align_bytes=64, name="w_perm")
+        s_perm = keep.tile([P, 4, N], U8, align_bytes=64, name="s_perm")
+        h_codes = keep.tile([P, 2, 2, TOK], U32, align_bytes=64, name="h_codes")
+        h_scales = keep.tile([P, 2, 2, TOK], U8, align_bytes=64, name="h_scales")
+        y_scales = keep.tile([P, 2, 4, TOK], U8, align_bytes=64, name="y_scales")
+        accs = [keep.tile([P, 4, 2, T], F32, name="acc%d" % i) for i in range(NA)]
+        fars = [keep.tile([P, 4, 2, T], F32, name="far%d" % i) for i in range(NF)]
+        inters = [keep.tile([P, TOK, 4], BF16, name="inter%d" % i, align_bytes=64) for i in range(2)]
+        ys = [keep.tile([P, 4, TOK], F32, name="y%d" % i) for i in range(NY)]
+        gates = [keep.tile([P, TOK], F32, name="gate%d" % i) for i in range(3)]
+        outs = [keep.tile([P, 4, 512], F32, name="o%d" % i) for i in range(NO)]
+        ybfs = [keep.tile([P, TOK, 4], BF16, name="ybf%d" % i, align_bytes=64) for i in range(NB)]
+        codes = [keep.tile([P, TOK], U32, name="codes%d" % i, align_bytes=64) for i in range(3)]
+        eng = {"V": nc.vector, "S": nc.scalar, "G": nc.gpsimd}
+
+        def load_x(h, g):
+            for b in range(2):
+                nc.sync.dma_start(
+                    out=x_sb[h][g][:, b, :, :],
+                    in_=x[2 * h + b, PAST:, 512 * g : 512 * (g + 1)].rearrange("(a p) c -> p a c", p=P),
+                )
+
+        def load_words(j0, j1):
+            cols = slice(1024 * j0, 1024 * j1)
+            for m in range(2):
+                nc.sync.dma_start(
+                    out=w_raw[:, 2 * m : 2 * m + 2, cols].bitcast(I32),
+                    in_=w_words[m].rearrange("g p w -> p g w")[:, :, cols].bitcast(I32),
+                )
+
+        def load_scales():
+            for m in range(2):
+                nc.sync.dma_start(out=s_raw[32 * m : 32 * (m + 1), :].bitcast(I32),
+                                  in_=w_scales[m].rearrange("g q n -> (g q) n").bitcast(I32))
+
+        def place_scales(i):
+            for q in range(4):
+                nc.sync.dma_start(
+                    out=s_perm[32 * q : 32 * q + 4, i, :].bitcast(I32),
+                    in_=s_mid[16 * i + 4 * q : 16 * i + 4 * q + 4, :].bitcast(I32),
+                )
+
+        def setup():
+            make_identity(nc, ident[:])
+            nc.vector.memset(s_raw[64:128, :].bitcast(I32), 0)
+            nc.vector.memset(hist[:].bitcast(I32), 0)
+            nc.vector.memset(warm[:], 0.0)
+            nc.vector.memset(brow[:].bitcast(I32), 0)
+            nc.scalar.dma_start(out=taps_raw[:], in_=taps.rearrange("j (g p t) -> p (j g) t", p=P, t=4))
+            nc.scalar.dma_start(out=hist[0:16, :], in_=x[:, 0:PAST, :])
+            nc.scalar.activation(out=warm_out[:], in_=warm[:], func=ACT.Sigmoid)
+
+        def clear_planes():
+            nc.vector.memset(s_perm[:].rearrange("p i n -> p (i n)").bitcast(I32), 0)
+
+        def load_bias():
+            for m, vec in enumerate((bg, bv)):
+                nc.sync.dma_start(out=bias_raw[m][:], in_=vec.rearrange("(j p t) -> p j t", p=P, t=4))
+
+        def load_brow():
+            for m, vec in enumerate((bg, bv)):
+                nc.sync.dma_start(out=brow[16 * m : 16 * (m + 1), :], in_=vec.rearrange("(a p) -> a p", p=P))
+
+        def cast_brow():
+            nc.scalar.copy(out=brow_f[:], in_=brow[:])
+
+        def turn_brow():
+            nc.tensor.transpose(banks[5][:, 0:P], brow_f[:], ident[:])
+
+        def copy_brow():
+            nc.scalar.copy(out=bias_n[:].rearrange("p m k -> p (m k)"), in_=banks[5][:, 0:32])
+
+        def cast_taps():
+            nc.vector.tensor_copy(out=taps_f[:].rearrange("p j k -> p (j k)"), in_=taps_raw[:].rearrange("p a t -> p (a t)"))
+
+        def cast_bias():
+            for m in range(2):
+                nc.scalar.copy(out=bias_f[:, m, :], in_=bias_raw[m][:].rearrange("p j t -> p (j t)"))
+
+        def perm_scales():
+            w = 512 * KB
+            if KB:
+                nc.vector.tensor_copy(out=s_mid[:, :w].bitcast(I32), in_=s_raw[:, :w].bitcast(I32))
+            if KB < 4:
+                nc.vector.tensor_copy(
+                    out=s_mid[:, w:].rearrange("p (j t c) -> p j t c", c=P, t=4),
+                    in_=s_raw[:, w:].rearrange("p (j c t) -> p j t c", c=P, t=4))
+
+        x_bank = {(0, 0): 0, (0, 1): 2, (1, 0): 6, (1, 1): 4}
+        acc_of = {(h, g): accs[(2 * h + g) % NA] for h in range(2) for g in range(2)}
+        far_of = {(h, g): fars[(2 * h + g) % NF] for h in range(2) for g in range(2)}
+
+        def turn_x(h, g, u):
+            words = x_sb[h][g][:].bitcast(F32)
+            for b in range(2):
+                for a in range(2):
+                    k = 2 * b + a
+                    nc.tensor.transpose(banks[x_bank[h, g] + u][:, P * k : P * (k + 1)], words[:, b, a, u:256:2], ident[:])
+
+        def turn_hist():
+            hist_words = hist[:].bitcast(F32)
+            for gu in range(4):
+                g, u = divmod(gu, 2)
+                nc.tensor.transpose(banks[4][:, P * gu : P * (gu + 1)], hist_words[:, 256 * g + u : 256 * (g + 1) : 2], ident[:])
+
+        def copy_hist():
+            nc.scalar.copy(out=hist_w[:], in_=banks[4][:].rearrange("p (k r) -> p k r", k=4)[:, :, 0:16])
+
+        def make_edge():
+            hist_b = hist_w[:].rearrange("p k r -> p (k r)").bitcast(BF16).rearrange("p (k n e) -> p k e n", k=4, e=2)
+            for dst, j in ((edge, 2), (edge1, 1)):
+                nc.gpsimd.tensor_tensor(
+                    out=dst[:].rearrange("p (k e) n -> p k e n", e=2), in0=hist_b,
+                    in1=taps_f[:, j, :].rearrange("p (k e) -> p k e", e=2).unsqueeze(3).to_broadcast([P, 4, 2, 16]),
+                    op=ALU.mult)
+            ev = edge[:].rearrange("p k (b r) -> p (k b) r", r=4)
+            e1v = edge1[:].rearrange("p k (b r) -> p (k b) r", r=4)
+            nc.gpsimd.tensor_tensor(out=ev[:, :, 0:2], in0=ev[:, :, 0:2], in1=e1v[:, :, 2:4], op=ALU.add)
+
+        def frames(h, g, t):
+            u, e = divmod(t, 2)
+            return banks[x_bank[h, g] + u][:].bitcast(BF16).rearrange("p (b r e) -> p b r e", b=2, e=2)[:, :, :, e]
+
+        def tap(j, g, t):
+            return taps_f[:, j, 4 * g + t : 4 * g + t + 1]
+
+        def edge_of(h, g):
+            return edge[:, 4 * g : 4 * g + 4, 8 * h : 8 * h + 8].rearrange("p t (b r) -> p t b r", b=2)
+
+        def lag0(h, g, t):
+            nc.scalar.activation(out=acc_of[h, g][:, t, :, :], in_=frames(h, g, t), func=ACT.Copy, scale=tap(0, g, t))
+
+        def lag1(h, g, t):
+            acc = acc_of[h, g]
+            nc.vector.scalar_tensor_tensor(
+                out=acc[:, t, :, 2:], in0=frames(h, g, t)[:, :, : T - 2], scalar=tap(1, g, t),
+                in1=acc[:, t, :, 2:], op0=ALU.mult, op1=ALU.add)
+
+        def far(h, g, t):
+            nc.scalar.activation(out=far_of[h, g][:, t, :, 4:], in_=frames(h, g, t)[:, :, : T - 4], func=ACT.Copy,
+                                 scale=tap(2, g, t))
+
+        def far_edge(h, g):
+            nc.scalar.copy(out=far_of[h, g][:, :, :, 0:4], in_=edge_of(h, g))
+
+        def add_far(e, hg, c0, c1):
+            h, g = divmod(hg, 2)
+            terms = [a[:].rearrange("p t b u -> p t (b u)")[:, :, c0:c1].rearrange("p t (c i) -> p c t i", i=4)
+                     for a in (acc_of[h, g], far_of[h, g])]
+            eng[e].tensor_tensor(out=inters[g][:, c0:c1, :].rearrange("p (c i) t -> p c t i", i=4),
+                                 in0=terms[0], in1=terms[1], op=ALU.add)
+
+        def interleave(e, dst, src, c0, c1):
+            o = dst[:, c0:c1, :].rearrange("p (c i) t -> p c t i", i=4)
+            s = src[:, :, c0:c1].rearrange("p t (c i) -> p c t i", i=4)
+            if e == "S":
+                nc.scalar.copy(out=o, in_=s)
+            elif e == "G":
+                nc.gpsimd.tensor_scalar(out=o, in0=s, scalar1=1.0, scalar2=-0.0, op0=ALU.mult, op1=ALU.add)
+            else:
+                nc.vector.tensor_copy(out=o, in_=s)
+
+        def quant_h(h, g):
+            nc.vector.quantize_mx(out=h_codes[:, h, g, :].bitcast(FP8X4), scales=h_scales[:, h, g, :],
+                                  in_=inters[g][:].rearrange("p n t -> p (n t)"))
+
+        def perm(k):
+            j, t = divmod(k, 4)
+            nc.vector.tensor_copy(
+                out=w_perm[:, k - 4 * KB, :, :].rearrange("p i (c e) -> p i c e", e=2),
+                in_=w_raw[:, :, 1024 * j : 1024 * (j + 1)].rearrange("p i (c t e) -> p i c t e", t=4, e=2)[:, :, :, t, :])
+
+        def stationary(j, t, i):
+            if j < KB:
+                return w_raw[:, i, 1024 * j + 256 * t : 1024 * j + 256 * (t + 1)]
+            return w_perm[:, 4 * (j - KB) + t, i, :]
+
+        def bias(m, n, t):
+            j = UNITS[n][1]
+            return (bias_n if j < KB else bias_f)[:, m, 4 * j + t : 4 * j + t + 1]
+
+        def slot(n, t, c0):
+            return 4 * n + t + (4 if HALF and n == 7 and c0 >= 256 else 0)
+
+        def passes(n, t, m, c0, c1, g0=0, g1=2):
+            h, j = UNITS[n]
+            acc = banks[(2 * slot(n, t, c0) + m) % 4]
+            for g in range(g0, g1):
+                i = 2 * m + g
+                nc.tensor.matmul_mx(
+                    out=acc[:, c0:c1], lhsT=stationary(j, t, i).bitcast(FP4X4),
+                    lhsT_scale=s_perm[:, i, 512 * j + P * t : 512 * j + P * (t + 1)],
+                    rhs=h_codes[:, h, g, c0:c1].bitcast(FP8X4), rhs_scale=h_scales[:, h, g, c0:c1],
+                    start=(g == 0), stop=(g == 1))
+
+        def mx(n, t, c0=0, c1=TOK, w=TOK):
+            for m in range(2):
+                for c in range(c0, c1, w):
+                    passes(n, t, m, c, c + w)
+
+        def gate(n, t, c0=0, c1=TOK):
+            nc.scalar.activation(out=gates[slot(n, t, c0) % 3][:, c0:c1], in_=banks[2 * slot(n, t, c0) % 4][:, c0:c1],
+                                 func=ACT.Sigmoid, bias=bias(0, n, t))
+
+        def value(n, t, c0=0, c1=TOK):
+            nc.vector.scalar_tensor_tensor(
+                out=ys[n % NY][:, t, c0:c1], in0=banks[(2 * slot(n, t, c0) + 1) % 4][:, c0:c1], scalar=bias(1, n, t),
+                in1=gates[slot(n, t, c0) % 3][:, c0:c1], op0=ALU.add, op1=ALU.mult)
+
+        def block(s):
+            if s < 32 and s > 1:
+                mx(*divmod(s, 4))
+            if 0 <= s - SKEW < 31:
+                gate(*divmod(s - SKEW, 4))
+                value(*divmod(s - SKEW, 4))
+
+        uses = []
+        for n in range(8):
+            uses.extend([("turn", n, k) for k in range(4)])
+            if UNITS[n][1] < KB:
+                uses.extend([("back", n, k) for k in range(2)])
+
+        def ring(kind, n, k):
+            i = uses.index((kind, n, k))
+            return banks[6 + i % 2] if i < EARLY else banks[4 + (i - EARLY) % 4]
+
+        def turn_bank(n, k):
+            return ring("turn", n, k)
+
+        def cast(e, n, c0, c1):
+            o = cbs[n % 2][:].rearrange("p u k (c e) -> p u (k c) e", e=2)[:, :, c0:c1, :]
+            s = outs[n % NO][:].rearrange("p k (c u e) -> p u (k c) e", u=2, e=2)[:, :, c0:c1, :]
+            if e == "S":
+                nc.scalar.copy(out=o, in_=s)
+            elif e == "G":
+                nc.gpsimd.tensor_scalar(out=o, in0=s, scalar1=1.0, scalar2=-0.0, op0=ALU.mult, op1=ALU.add)
+            else:
+                nc.vector.tensor_copy(out=o, in_=s)
+
+        def back(n, half):
+            words = cbs[n % 2][:].bitcast(F32)
+            for u in range(2):
+                for a in range(2):
+                    nc.tensor.transpose(ring("back", n, half)[:, 256 * u + P * a : 256 * u + P * (a + 1)],
+                                        words[:, u, 2 * half + a, :], ident[:])
+
+        def evac(e, n, half):
+            o = ybfs[n % NB][:, 256 * half : 256 * (half + 1), :].bitcast(F32)
+            s = ring("back", n, half)[:].rearrange("p (u r) -> p r u", u=2)
+            if e == "S":
+                nc.scalar.copy(out=o, in_=s)
+            else:
+                nc.vector.tensor_copy(out=o, in_=s)
+
+        def turn(n, k, t0=0, t1=4):
+            for t in range(t0, t1):
+                nc.tensor.transpose(turn_bank(n, k)[:, P * t : P * (t + 1)], ys[n % NY][:, t, P * k : P * (k + 1)], ident[:])
+
+        def drain(e, n, k):
+            o = outs[n % NO][:, k, :]
+            s = turn_bank(n, k)[:]
+            if UNITS[n][1] >= KB:
+                o = o.rearrange("p (c t) -> p c t", t=4)
+                s = s.rearrange("p (t c) -> p c t", t=4)
+            if e == "S":
+                nc.scalar.copy(out=o, in_=s)
+            else:
+                nc.vector.tensor_copy(out=o, in_=s)
+
+        def store_y(n, k0, k1):
+            h, j = UNITS[n]
+            nc.sync.dma_start(
+                out=y_rows[TOK * h + P * k0 : TOK * h + P * k1, 512 * j : 512 * (j + 1)].rearrange("(k p) n -> p k n", p=P),
+                in_=outs[n % NO][:, k0:k1, :])
+
+        def inter_y(e, n, c0, c1):
+            interleave(e, ybfs[n % NB], ys[n % NY][:], c0, c1)
+
+        def quant_y(n, c0, c1):
+            h, j = UNITS[n]
+            nc.vector.quantize_mx(out=codes[n % 3][:, c0:c1].bitcast(FP8X4), scales=y_scales[:, h, j, c0:c1],
+                                  in_=ybfs[n % NB][:, c0:c1, :].rearrange("p n t -> p (n t)"))
+
+        def store_codes(n, c0, c1):
+            h, j = UNITS[n]
+            nc.sync.dma_start(
+                out=out_1[j, :, TOK * h + c0 : TOK * h + c1, :].rearrange("p n t -> p (n t)").bitcast(I32),
+                in_=codes[n % 3][:, c0:c1].bitcast(I32))
+
+        def store_scales(h, q, j0=0, j1=4):
+            nc.sync.dma_start(
+                out=out_2[j0:j1, 4 * q : 4 * q + 4, TOK * h : TOK * (h + 1)].rearrange("j r n -> r j n").bitcast(I32),
+                in_=y_scales[32 * q : 32 * q + 4, h, j0:j1, :].bitcast(I32))
+
+        steps = dict(
+            setup=setup, clear_planes=clear_planes, block=block, load_brow=load_brow, cast_brow=cast_brow, turn_brow=turn_brow, copy_brow=copy_brow,
+            cast=cast, back=back, evac=evac, load_bias=load_bias, load_x=load_x, load_words=load_words, load_scales=load_scales, place_scales=place_scales,
+            cast_taps=cast_taps, cast_bias=cast_bias, perm_scales=perm_scales, turn_x=turn_x, turn_hist=turn_hist,
+            copy_hist=copy_hist, make_edge=make_edge, lag0=lag0, lag1=lag1, far=far, far_edge=far_edge, add_far=add_far,
+            quant_h=quant_h, perm=perm, passes=passes, mx=mx,
+            gate=gate, value=value, turn=turn, drain=drain, store_y=store_y, inter_y=inter_y, quant_y=quant_y,
+            store_codes=store_codes, store_scales=store_scales)
+        for step in PLAN:
+            steps[step[0]](*step[1:])

@@ -18,7 +18,7 @@ FLOPS = 2 * 2 * B * T * C * N
 P = 128
 TOK = 512
 NY = 4
-KB = 1
+KB = 0
 EARLY = 4
 HALF = False
 NO = 3
@@ -28,62 +28,67 @@ NF = 2
 NB = 3
 UNITS = [(h, j) for h in range(2) for j in range(4)]
 PLAN = [
-    ("setup",), ("load_x", 0, 0), ("cast_taps",), ("turn_x", 0, 0, 0), ("turn_x", 0, 0, 1), ("lag0", 0, 0, 0),
-    ("load_scales",), ("load_x", 0, 1), ("load_words", 0, 1), ("lag0", 0, 0, 1), ("load_words", 1, 2),
-    ("turn_x", 0, 1, 0), ("clear_planes",), ("turn_x", 0, 1, 1), ("perm_scales",), ("load_x", 1, 0), ("load_brow",),
-    ("lag1", 0, 0, 0), ("lag0", 0, 0, 2), ("lag0", 0, 0, 3), ("lag0", 0, 1, 0), ("load_bias",), ("lag0", 0, 1, 1),
-    ("load_words", 2, 3), ("lag1", 0, 0, 1), ("far", 0, 0, 0), ("lag1", 0, 0, 2), ("place_scales", 0),
-    ("turn_hist",), ("lag0", 0, 1, 2), ("copy_hist",), ("lag0", 0, 1, 3), ("lag1", 0, 0, 3), ("far", 0, 0, 1),
-    ("lag1", 0, 1, 0), ("perm", 4), ("lag1", 0, 1, 1), ("far", 0, 0, 2), ("make_edge",), ("far", 0, 0, 3),
-    ("place_scales", 2), ("far_edge", 0, 0), ("lag1", 0, 1, 2), ("cast_brow",), ("turn_x", 1, 0, 0), ("turn_brow",),
-    ("far_edge", 0, 1), ("turn_x", 1, 0, 1), ("far", 0, 1, 0), ("copy_brow",), ("place_scales", 1),
-    ("lag1", 0, 1, 3), ("perm", 5), ("far", 0, 1, 1), ("far", 0, 1, 2), ("add_far", "V", 0, 0, 512),
-    ("load_x", 1, 1), ("far", 0, 1, 3), ("lag0", 1, 0, 0), ("perm", 6), ("quant_h", 0, 0), ("far_edge", 1, 0),
-    ("passes", 0, 0, 0, 0, 512, 0, 1), ("passes", 0, 0, 1, 0, 512, 0, 1), ("add_far", "V", 1, 0, 512),
-    ("far", 1, 0, 0), ("passes", 0, 1, 0, 0, 512, 0, 1), ("perm", 7), ("lag0", 1, 0, 1), ("turn_x", 1, 1, 0),
-    ("turn_x", 1, 1, 1), ("quant_h", 0, 1), ("lag0", 1, 0, 2), ("lag0", 1, 0, 3), ("cast_bias",), ("far", 1, 0, 1),
-    ("lag0", 1, 1, 0), ("passes", 0, 1, 1, 0, 512, 0, 1), ("place_scales", 3), ("passes", 0, 0, 0, 0, 512, 1, 2),
-    ("lag1", 1, 0, 0), ("far", 1, 0, 2), ("passes", 0, 0, 1, 0, 512, 1, 2), ("passes", 0, 1, 0, 0, 512, 1, 2),
-    ("load_words", 3, 4), ("lag1", 1, 0, 1), ("passes", 0, 1, 1, 0, 512, 1, 2), ("lag1", 1, 0, 2), ("block", 1),
-    ("block", 2), ("perm", 8), ("lag0", 1, 1, 1), ("block", 3), ("far", 1, 0, 3), ("lag0", 1, 1, 2),
-    ("lag1", 1, 0, 3), ("lag1", 1, 1, 0), ("block", 4), ("lag0", 1, 1, 3), ("perm", 9), ("block", 5),
-    ("turn", 0, 0), ("turn", 0, 1), ("far_edge", 1, 1), ("block", 6), ("add_far", "V", 2, 0, 512), ("far", 1, 1, 0),
-    ("drain", "S", 0, 0), ("drain", "S", 0, 1), ("block", 7), ("far", 1, 1, 1), ("perm", 10), ("turn", 0, 2),
-    ("turn", 0, 3), ("block", 8), ("lag1", 1, 1, 1), ("far", 1, 1, 2), ("drain", "S", 0, 2), ("block", 9),
-    ("far", 1, 1, 3), ("perm", 11), ("block", 10), ("drain", "S", 0, 3), ("perm", 12), ("lag1", 1, 1, 2),
-    ("block", 11), ("lag1", 1, 1, 3), ("cast", "S", 0, 0, 512), ("turn", 1, 0), ("perm", 13), ("quant_h", 1, 0),
-    ("block", 12), ("turn", 1, 1), ("perm", 14), ("back", 0, 0), ("back", 0, 1), ("block", 13), ("evac", "S", 0, 0),
-    ("turn", 1, 2), ("evac", "S", 0, 1), ("drain", "S", 1, 0), ("turn", 1, 3), ("store_y", 0, 0, 2),
-    ("drain", "S", 1, 1), ("drain", "S", 1, 2), ("drain", "S", 1, 3), ("perm", 15), ("add_far", "V", 3, 0, 512),
-    ("block", 14), ("store_y", 0, 2, 4), ("turn", 2, 0), ("turn", 2, 1), ("turn", 2, 2), ("store_y", 1, 0, 2),
-    ("quant_h", 1, 1), ("turn", 2, 3), ("block", 15), ("drain", "S", 2, 0), ("block", 16), ("drain", "S", 2, 1),
-    ("inter_y", "V", 1, 0, 512), ("block", 17), ("quant_y", 0, 0, 512), ("drain", "S", 2, 2), ("turn", 3, 0),
-    ("quant_y", 1, 0, 512), ("turn", 3, 1), ("store_y", 1, 2, 4), ("drain", "S", 2, 3), ("turn", 3, 2),
-    ("turn", 3, 3), ("block", 18), ("store_codes", 0, 0, 512), ("drain", "S", 3, 0), ("store_y", 2, 0, 2),
-    ("drain", "S", 3, 1), ("block", 19), ("drain", "V", 3, 2), ("drain", "S", 3, 3), ("block", 20),
-    ("inter_y", "V", 2, 0, 512), ("quant_y", 2, 0, 512), ("block", 21), ("turn", 4, 0), ("store_y", 2, 2, 4),
-    ("drain", "V", 4, 0), ("inter_y", "S", 3, 0, 512), ("turn", 4, 1), ("turn", 4, 2), ("turn", 4, 3),
-    ("block", 22), ("block", 23), ("drain", "V", 4, 1), ("drain", "S", 4, 2), ("block", 24),
-    ("store_codes", 1, 0, 512), ("store_y", 3, 0, 2), ("drain", "S", 4, 3), ("cast", "V", 4, 0, 512),
-    ("store_codes", 2, 0, 512), ("block", 25), ("store_y", 3, 2, 4), ("turn", 5, 0), ("quant_y", 3, 0, 512),
-    ("turn", 5, 1), ("back", 4, 0), ("back", 4, 1), ("store_y", 4, 0, 2), ("block", 26), ("drain", "S", 5, 0),
-    ("drain", "S", 5, 1), ("evac", "S", 4, 0), ("inter_y", "V", 5, 0, 512), ("store_y", 4, 2, 4),
-    ("evac", "S", 4, 1), ("store_codes", 3, 0, 512), ("quant_y", 4, 0, 512), ("block", 27), ("turn", 5, 2),
-    ("turn", 5, 3), ("store_y", 5, 0, 2), ("block", 28), ("store_scales", 0, 0), ("turn", 6, 0),
-    ("drain", "S", 5, 2), ("turn", 6, 1), ("turn", 6, 2), ("store_scales", 0, 1), ("quant_y", 5, 0, 512),
-    ("drain", "S", 5, 3), ("inter_y", "V", 6, 0, 512), ("store_scales", 0, 2), ("turn", 6, 3), ("block", 29),
-    ("drain", "S", 6, 0), ("quant_y", 6, 0, 512), ("drain", "S", 6, 1), ("drain", "V", 6, 2), ("drain", "S", 6, 3),
-    ("block", 30), ("store_scales", 0, 3), ("block", 31), ("store_codes", 4, 0, 512), ("store_codes", 5, 0, 512),
-    ("gate", 7, 3), ("value", 7, 3, 0, 128), ("value", 7, 3, 128, 256), ("turn", 7, 0, 0, 3), ("turn", 7, 0, 3, 4),
-    ("drain", "S", 7, 0), ("value", 7, 3, 256, 384), ("turn", 7, 1, 0, 3), ("store_y", 5, 2, 4),
-    ("store_y", 6, 0, 2), ("store_scales", 1, 0, 0, 3), ("turn", 7, 1, 3, 4), ("store_y", 6, 2, 4),
-    ("store_scales", 1, 1, 0, 3), ("turn", 7, 2, 0, 3), ("store_codes", 6, 0, 512), ("store_scales", 1, 2, 0, 3),
-    ("drain", "S", 7, 1), ("store_scales", 1, 3, 0, 3), ("value", 7, 3, 384, 512), ("inter_y", "V", 7, 0, 256),
-    ("store_y", 7, 0, 1), ("turn", 7, 2, 3, 4), ("quant_y", 7, 0, 256), ("drain", "S", 7, 2),
-    ("inter_y", "V", 7, 256, 512), ("store_codes", 7, 0, 256), ("store_y", 7, 1, 2), ("turn", 7, 3, 0, 3),
-    ("store_y", 7, 2, 3), ("quant_y", 7, 256, 512), ("store_scales", 1, 0, 3, 4), ("store_scales", 1, 1, 3, 4),
-    ("store_scales", 1, 2, 3, 4), ("turn", 7, 3, 3, 4), ("drain", "S", 7, 3), ("store_y", 7, 3, 4),
-    ("store_scales", 1, 3, 3, 4), ("store_codes", 7, 256, 512),
+    ("load_x", 0, 0), ("setup",), ("turn_x", 0, 0, 0), ("cast_taps",), ("lag0", 0, 0, 0), ("far", 0, 0, 0),
+    ("turn_x", 0, 0, 1), ("turn_hist",), ("far", 0, 0, 1), ("load_scales",), ("clear_planes",), ("lag0", 0, 0, 1),
+    ("load_words", 0, 1), ("far", 0, 0, 2), ("load_bias",), ("perm_scales",), ("perm", 0), ("lag0", 0, 0, 2),
+    ("copy_hist",), ("load_x", 0, 1), ("lag0", 0, 0, 3), ("far", 0, 0, 3), ("perm", 1), ("make_edge",),
+    ("load_x", 1, 0), ("perm", 2), ("turn_x", 0, 1, 0), ("perm", 3), ("place_scales", 0), ("lag1", 0, 0, 0),
+    ("lag0", 0, 1, 0), ("lag0", 0, 1, 1), ("far_edge", 0, 0), ("lag1", 0, 0, 1), ("turn_x", 0, 1, 1),
+    ("place_scales", 2), ("lag1", 0, 0, 2), ("lag1", 0, 0, 3), ("far_edge", 1, 0), ("lag0", 0, 1, 2),
+    ("lag1", 0, 1, 0), ("lag1", 0, 1, 1), ("load_x", 1, 1), ("place_scales", 1), ("lag0", 0, 1, 3),
+    ("lag2", 0, 1, 0), ("load_words", 1, 2), ("turn_x", 1, 0, 0), ("add_far", "G", 0, 0, 128), ("lag0", 1, 0, 0),
+    ("lag0", 1, 0, 1), ("far", 1, 0, 0), ("add_far", "G", 0, 128, 256), ("far", 1, 0, 1), ("turn_x", 1, 0, 1),
+    ("lag1", 0, 1, 2), ("lag1", 0, 1, 3), ("lag2", 0, 1, 1), ("lag2", 0, 1, 3), ("lag0", 1, 0, 2),
+    ("turn_x", 1, 1, 0), ("lag0", 1, 0, 3), ("lag2", 0, 1, 2), ("far", 1, 0, 2), ("far", 1, 0, 3), ("cast_bias",),
+    ("lag1", 1, 0, 0), ("place_scales", 3), ("add_far", "V", 0, 256, 384), ("inter_h", "S", 1, 384, 512),
+    ("add_far", "G", 0, 384, 512), ("fix_edge", 0, 1), ("inter_h", "G", 1, 0, 128), ("quant_h", 0, 0),
+    ("lag1", 1, 0, 1), ("passes", 0, 0, 0, 0, 512, 0, 1), ("inter_h", "S", 1, 256, 384),
+    ("inter_h", "S", 1, 128, 256), ("passes", 0, 0, 1, 0, 512, 0, 1), ("lag1", 1, 0, 2), ("load_words", 2, 3),
+    ("far", 1, 1, 0), ("passes", 0, 1, 0, 0, 512, 0, 1), ("lag0", 1, 1, 0), ("passes", 0, 1, 1, 0, 512, 0, 1),
+    ("lag1", 1, 0, 3), ("quant_h", 0, 1), ("perm", 4), ("perm", 5), ("load_words", 3, 4), ("perm", 6),
+    ("passes", 0, 0, 0, 0, 512, 1, 2), ("add_far", "G", 2, 0, 128), ("lag0", 1, 1, 1),
+    ("passes", 0, 0, 1, 0, 512, 1, 2), ("passes", 0, 1, 0, 0, 512, 1, 2), ("far", 1, 1, 1), ("block", 1),
+    ("passes", 0, 1, 1, 0, 512, 1, 2), ("turn_x", 1, 1, 1), ("block", 2), ("far", 1, 1, 2), ("perm", 7),
+    ("block", 3), ("lag1", 1, 1, 0), ("lag0", 1, 1, 2), ("block", 4), ("lag0", 1, 1, 3), ("lag1", 1, 1, 1),
+    ("block", 5), ("turn", 0, 0), ("far", 1, 1, 3), ("lag1", 1, 1, 2), ("turn", 0, 1), ("lag1", 1, 1, 3),
+    ("block", 6), ("drain", "S", 0, 0), ("perm", 8), ("drain", "S", 0, 1), ("turn", 0, 2), ("far_edge", 1, 1),
+    ("perm", 9), ("turn", 0, 3), ("block", 7), ("add_far", "G", 2, 128, 256), ("add_far", "G", 2, 256, 384),
+    ("add_far", "G", 2, 384, 512), ("inter_y", "S", 0, 0, 256), ("block", 8), ("perm", 10), ("drain", "S", 0, 2),
+    ("block", 9), ("turn", 1, 0), ("turn", 1, 1), ("drain", "S", 0, 3), ("turn", 1, 2), ("turn", 1, 3),
+    ("block", 10), ("perm", 11), ("add_far", "G", 3, 0, 128), ("perm", 12), ("store_y", 0, 0, 2),
+    ("inter_y", "S", 0, 256, 512), ("inter_y", "S", 1, 0, 256), ("perm", 13), ("block", 11), ("block", 12),
+    ("drain", "S", 1, 0), ("perm", 14), ("add_far", "G", 3, 128, 256), ("block", 13), ("drain", "S", 1, 1),
+    ("block", 14), ("turn", 2, 0), ("perm", 15), ("drain", "S", 1, 2), ("store_y", 0, 2, 4),
+    ("add_far", "G", 3, 256, 384), ("add_far", "G", 3, 384, 512), ("turn", 2, 1), ("turn", 2, 2), ("quant_h", 1, 0),
+    ("quant_h", 1, 1), ("drain", "S", 1, 3), ("turn", 2, 3), ("block", 15), ("inter_y", "S", 1, 256, 512),
+    ("block", 16), ("drain", "V", 2, 0), ("drain", "S", 2, 1), ("block", 17), ("block", 18), ("drain", "S", 2, 2),
+    ("quant_y", 0, 0, 512), ("drain", "S", 2, 3), ("inter_y", "G", 2, 0, 256), ("block", 19), ("store_y", 1, 0, 2),
+    ("turn", 3, 0), ("turn", 3, 1), ("drain", "V", 3, 0), ("turn", 3, 2), ("turn", 3, 3), ("block", 20),
+    ("drain", "V", 3, 1), ("inter_y", "V", 2, 256, 512), ("inter_y", "S", 3, 0, 256), ("store_y", 1, 2, 4),
+    ("block", 21), ("inter_y", "G", 3, 256, 512), ("store_y", 2, 0, 2), ("quant_y", 1, 0, 512), ("turn", 4, 0),
+    ("quant_y", 2, 0, 512), ("turn", 4, 1), ("store_codes", 0, 0, 512), ("quant_y", 3, 0, 512),
+    ("drain", "S", 3, 2), ("drain", "S", 3, 3), ("turn", 4, 2), ("inter_y", "G", 4, 0, 256), ("turn", 4, 3),
+    ("block", 22), ("inter_y", "S", 4, 256, 512), ("block", 23), ("drain", "V", 4, 0), ("block", 24),
+    ("store_y", 2, 2, 4), ("drain", "S", 4, 1), ("store_y", 3, 0, 2), ("store_codes", 1, 0, 512),
+    ("store_scales", 0, 0), ("inter_y", "V", 5, 0, 256), ("store_y", 3, 2, 4), ("block", 25), ("drain", "S", 4, 2),
+    ("store_codes", 2, 0, 512), ("store_codes", 3, 0, 512), ("turn", 5, 0), ("turn", 5, 1), ("turn", 5, 2),
+    ("drain", "S", 4, 3), ("turn", 5, 3), ("store_y", 4, 0, 2), ("inter_y", "G", 5, 256, 512), ("drain", "V", 5, 0),
+    ("block", 26), ("drain", "S", 5, 1), ("quant_y", 4, 0, 512), ("drain", "S", 5, 2), ("quant_y", 5, 0, 512),
+    ("block", 27), ("block", 28), ("store_y", 4, 2, 4), ("drain", "S", 5, 3), ("turn", 6, 0), ("turn", 6, 1),
+    ("store_scales", 0, 1), ("drain", "V", 6, 0), ("store_y", 5, 0, 2), ("drain", "V", 6, 1),
+    ("inter_y", "G", 6, 0, 256), ("turn", 6, 2), ("store_scales", 0, 2), ("turn", 6, 3), ("block", 29),
+    ("inter_y", "S", 6, 256, 512), ("quant_y", 6, 0, 512), ("block", 30), ("drain", "S", 6, 2),
+    ("drain", "V", 6, 3), ("store_codes", 4, 0, 512), ("block", 31), ("turn", 7, 0, 0, 3), ("gate", 7, 3),
+    ("value", 7, 3, 0, 128), ("value", 7, 3, 128, 256), ("store_codes", 5, 0, 512), ("turn", 7, 0, 3, 4),
+    ("turn", 7, 1, 0, 3), ("store_scales", 0, 3), ("drain", "S", 7, 0), ("store_y", 5, 2, 4),
+    ("value", 7, 3, 256, 384), ("turn", 7, 1, 3, 4), ("store_y", 6, 0, 2), ("turn", 7, 2, 0, 3),
+    ("store_codes", 6, 0, 512), ("store_scales", 1, 0, 0, 3), ("store_y", 6, 2, 4), ("store_scales", 1, 1, 0, 3),
+    ("store_scales", 1, 2, 0, 3), ("inter_y", "V", 7, 0, 256), ("store_scales", 1, 3, 0, 3),
+    ("value", 7, 3, 384, 512), ("store_y", 7, 0, 1), ("quant_y", 7, 0, 256), ("turn", 7, 2, 3, 4),
+    ("store_codes", 7, 0, 256), ("turn", 7, 3, 0, 3), ("drain", "S", 7, 1), ("store_y", 7, 1, 2),
+    ("inter_y", "V", 7, 256, 512), ("quant_y", 7, 256, 512), ("drain", "S", 7, 2), ("turn", 7, 3, 3, 4),
+    ("drain", "S", 7, 3), ("store_y", 7, 2, 3), ("store_scales", 1, 0, 3, 4), ("store_scales", 1, 1, 3, 4),
+    ("store_scales", 1, 2, 3, 4), ("store_y", 7, 3, 4), ("store_scales", 1, 3, 3, 4), ("store_codes", 7, 256, 512),
 ]
 
 
@@ -114,10 +119,6 @@ def tile_lag_mix_gated_channels_g4_kernel(
         edge1 = keep.tile([P, 8, 16], F32, name="edge1")
         edge = keep.tile([P, 8, 16], F32, name="edge")
         w_raw = keep.tile([P, 4, 4096], U8, name="w_raw", align_bytes=64)
-        brow = keep.tile([P, P], BF16, name="brow")
-        brow_f = keep.tile([P, P], F32, name="brow_f")
-        bias_n = keep.tile([P, 2, 16], F32, name="bias_n")
-        cbs = [keep.tile([P, 2, 4, 256], BF16, name="cb%d" % i) for i in range(2)]
         s_raw = keep.tile([P, N], U8, name="s_raw")
         s_mid = keep.tile([P, N], U8, name="s_mid")
         w_perm = keep.tile([P, max(16 - 4 * KB, 1), 4, 256], U8, align_bytes=64, name="w_perm")
@@ -127,6 +128,7 @@ def tile_lag_mix_gated_channels_g4_kernel(
         y_scales = keep.tile([P, 2, 4, TOK], U8, align_bytes=64, name="y_scales")
         accs = [keep.tile([P, 4, 2, T], F32, name="acc%d" % i) for i in range(NA)]
         fars = [keep.tile([P, 4, 2, T], F32, name="far%d" % i) for i in range(NF)]
+        rows = keep.tile([P, 4, 2, T], BF16, name="rows")
         inters = [keep.tile([P, TOK, 4], BF16, name="inter%d" % i, align_bytes=64) for i in range(2)]
         ys = [keep.tile([P, 4, TOK], F32, name="y%d" % i) for i in range(NY)]
         gates = [keep.tile([P, TOK], F32, name="gate%d" % i) for i in range(3)]
@@ -167,7 +169,6 @@ def tile_lag_mix_gated_channels_g4_kernel(
             nc.vector.memset(s_raw[64:128, :].bitcast(I32), 0)
             nc.vector.memset(hist[:].bitcast(I32), 0)
             nc.vector.memset(warm[:], 0.0)
-            nc.vector.memset(brow[:].bitcast(I32), 0)
             nc.scalar.dma_start(out=taps_raw[:], in_=taps.rearrange("j (g p t) -> p (j g) t", p=P, t=4))
             nc.scalar.dma_start(out=hist[0:16, :], in_=x[:, 0:PAST, :])
             nc.scalar.activation(out=warm_out[:], in_=warm[:], func=ACT.Sigmoid)
@@ -178,19 +179,6 @@ def tile_lag_mix_gated_channels_g4_kernel(
         def load_bias():
             for m, vec in enumerate((bg, bv)):
                 nc.sync.dma_start(out=bias_raw[m][:], in_=vec.rearrange("(j p t) -> p j t", p=P, t=4))
-
-        def load_brow():
-            for m, vec in enumerate((bg, bv)):
-                nc.sync.dma_start(out=brow[16 * m : 16 * (m + 1), :], in_=vec.rearrange("(a p) -> a p", p=P))
-
-        def cast_brow():
-            nc.scalar.copy(out=brow_f[:], in_=brow[:])
-
-        def turn_brow():
-            nc.tensor.transpose(banks[5][:, 0:P], brow_f[:], ident[:])
-
-        def copy_brow():
-            nc.scalar.copy(out=bias_n[:].rearrange("p m k -> p (m k)"), in_=banks[5][:, 0:32])
 
         def cast_taps():
             nc.vector.tensor_copy(out=taps_f[:].rearrange("p j k -> p (j k)"), in_=taps_raw[:].rearrange("p a t -> p (a t)"))
@@ -210,7 +198,7 @@ def tile_lag_mix_gated_channels_g4_kernel(
 
         x_bank = {(0, 0): 0, (0, 1): 2, (1, 0): 6, (1, 1): 4}
         acc_of = {(h, g): accs[(2 * h + g) % NA] for h in range(2) for g in range(2)}
-        far_of = {(h, g): fars[(2 * h + g) % NF] for h in range(2) for g in range(2)}
+        far_of = {(0, 0): fars[0], (1, 0): fars[1], (1, 1): fars[0]}
 
         def turn_x(h, g, u):
             words = x_sb[h][g][:].bitcast(F32)
@@ -258,6 +246,17 @@ def tile_lag_mix_gated_channels_g4_kernel(
                 out=acc[:, t, :, 2:], in0=frames(h, g, t)[:, :, : T - 2], scalar=tap(1, g, t),
                 in1=acc[:, t, :, 2:], op0=ALU.mult, op1=ALU.add)
 
+        def lag2(h, g, t):
+            nc.vector.scalar_tensor_tensor(
+                out=rows[:, t, :, 4:], in0=frames(h, g, t)[:, :, : T - 4], scalar=tap(2, g, t),
+                in1=acc_of[h, g][:, t, :, 4:], op0=ALU.mult, op1=ALU.add)
+
+        def fix_edge(h, g):
+            nc.vector.tensor_tensor(out=rows[:, :, :, 0:4], in0=acc_of[h, g][:, :, :, 0:4], in1=edge_of(h, g), op=ALU.add)
+
+        def inter_h(e, g, c0, c1):
+            interleave(e, inters[g], rows[:].rearrange("p t b u -> p t (b u)"), c0, c1)
+
         def far(h, g, t):
             nc.scalar.activation(out=far_of[h, g][:, t, :, 4:], in_=frames(h, g, t)[:, :, : T - 4], func=ACT.Copy,
                                  scale=tap(2, g, t))
@@ -267,14 +266,15 @@ def tile_lag_mix_gated_channels_g4_kernel(
 
         def add_far(e, hg, c0, c1):
             h, g = divmod(hg, 2)
-            terms = [a[:].rearrange("p t b u -> p t (b u)")[:, :, c0:c1].rearrange("p t (c i) -> p c t i", i=4)
+            terms = [a[:].rearrange("p t b u -> p t (b u)")[:, :, c0:c1].rearrange("p t (c i) -> p c t i", i=2)
                      for a in (acc_of[h, g], far_of[h, g])]
-            eng[e].tensor_tensor(out=inters[g][:, c0:c1, :].rearrange("p (c i) t -> p c t i", i=4),
+            eng[e].tensor_tensor(out=inters[g][:, c0:c1, :].rearrange("p (c i) t -> p c t i", i=2),
                                  in0=terms[0], in1=terms[1], op=ALU.add)
 
         def interleave(e, dst, src, c0, c1):
-            o = dst[:, c0:c1, :].rearrange("p (c i) t -> p c t i", i=4)
-            s = src[:, :, c0:c1].rearrange("p t (c i) -> p c t i", i=4)
+            run = 2 if e == "G" else 4
+            o = dst[:, c0:c1, :].rearrange("p (c i) t -> p c t i", i=run)
+            s = src[:, :, c0:c1].rearrange("p t (c i) -> p c t i", i=run)
             if e == "S":
                 nc.scalar.copy(out=o, in_=s)
             elif e == "G":
@@ -299,7 +299,7 @@ def tile_lag_mix_gated_channels_g4_kernel(
 
         def bias(m, n, t):
             j = UNITS[n][1]
-            return (bias_n if j < KB else bias_f)[:, m, 4 * j + t : 4 * j + t + 1]
+            return bias_f[:, m, 4 * j + t : 4 * j + t + 1]
 
         def slot(n, t, c0):
             return 4 * n + t + (4 if HALF and n == 7 and c0 >= 256 else 0)
@@ -349,31 +349,6 @@ def tile_lag_mix_gated_channels_g4_kernel(
         def turn_bank(n, k):
             return ring("turn", n, k)
 
-        def cast(e, n, c0, c1):
-            o = cbs[n % 2][:].rearrange("p u k (c e) -> p u (k c) e", e=2)[:, :, c0:c1, :]
-            s = outs[n % NO][:].rearrange("p k (c u e) -> p u (k c) e", u=2, e=2)[:, :, c0:c1, :]
-            if e == "S":
-                nc.scalar.copy(out=o, in_=s)
-            elif e == "G":
-                nc.gpsimd.tensor_scalar(out=o, in0=s, scalar1=1.0, scalar2=-0.0, op0=ALU.mult, op1=ALU.add)
-            else:
-                nc.vector.tensor_copy(out=o, in_=s)
-
-        def back(n, half):
-            words = cbs[n % 2][:].bitcast(F32)
-            for u in range(2):
-                for a in range(2):
-                    nc.tensor.transpose(ring("back", n, half)[:, 256 * u + P * a : 256 * u + P * (a + 1)],
-                                        words[:, u, 2 * half + a, :], ident[:])
-
-        def evac(e, n, half):
-            o = ybfs[n % NB][:, 256 * half : 256 * (half + 1), :].bitcast(F32)
-            s = ring("back", n, half)[:].rearrange("p (u r) -> p r u", u=2)
-            if e == "S":
-                nc.scalar.copy(out=o, in_=s)
-            else:
-                nc.vector.tensor_copy(out=o, in_=s)
-
         def turn(n, k, t0=0, t1=4):
             for t in range(t0, t1):
                 nc.tensor.transpose(turn_bank(n, k)[:, P * t : P * (t + 1)], ys[n % NY][:, t, P * k : P * (k + 1)], ident[:])
@@ -415,8 +390,7 @@ def tile_lag_mix_gated_channels_g4_kernel(
                 in_=y_scales[32 * q : 32 * q + 4, h, j0:j1, :].bitcast(I32))
 
         steps = dict(
-            setup=setup, clear_planes=clear_planes, block=block, load_brow=load_brow, cast_brow=cast_brow, turn_brow=turn_brow, copy_brow=copy_brow,
-            cast=cast, back=back, evac=evac, load_bias=load_bias, load_x=load_x, load_words=load_words, load_scales=load_scales, place_scales=place_scales,
+            setup=setup, lag2=lag2, fix_edge=fix_edge, inter_h=inter_h, clear_planes=clear_planes, block=block,  load_bias=load_bias, load_x=load_x, load_words=load_words, load_scales=load_scales, place_scales=place_scales,
             cast_taps=cast_taps, cast_bias=cast_bias, perm_scales=perm_scales, turn_x=turn_x, turn_hist=turn_hist,
             copy_hist=copy_hist, make_edge=make_edge, lag0=lag0, lag1=lag1, far=far, far_edge=far_edge, add_far=add_far,
             quant_h=quant_h, perm=perm, passes=passes, mx=mx,

from contextlib import ExitStack

import concourse.mybir as mybir
from concourse.masks import make_identity

F32 = mybir.dt.float32
BF16 = mybir.dt.bfloat16
I32 = mybir.dt.int32
U32 = mybir.dt.uint32
U8 = mybir.dt.uint8
FP8X4 = mybir.dt.float8_e4m3fn_x4
FP4X4 = mybir.dt.float4_e2m1fn_x4
ACT = mybir.ActivationFunctionType
ALU = mybir.AluOpType

B, T, C, N, PAST = 4, 256, 1024, 2048, 4
FLOPS = 2 * 2 * B * T * C * N
P = 128
TOK = 512
NY = 4
KB = 0
EARLY = 4
HALF = False
NO = 3
SKEW = 1
NA = 3
NF = 2
NB = 3
UNITS = [(h, j) for h in range(2) for j in range(4)]
PLAN = [
    ("load_x", 0, 0), ("setup",), ("turn_x", 0, 0, 0), ("cast_taps",), ("lag0", 0, 0, 0), ("far", 0, 0, 0),
    ("turn_x", 0, 0, 1), ("turn_hist",), ("far", 0, 0, 1), ("load_scales",), ("clear_planes",), ("lag0", 0, 0, 1),
    ("load_words", 0, 1), ("far", 0, 0, 2), ("load_bias",), ("perm_scales",), ("perm", 0), ("lag0", 0, 0, 2),
    ("copy_hist",), ("load_x", 0, 1), ("lag0", 0, 0, 3), ("far", 0, 0, 3), ("perm", 1), ("make_edge",),
    ("load_x", 1, 0), ("perm", 2), ("turn_x", 0, 1, 0), ("perm", 3), ("place_scales", 0), ("lag1", 0, 0, 0),
    ("lag0", 0, 1, 0), ("lag0", 0, 1, 1), ("far_edge", 0, 0), ("lag1", 0, 0, 1), ("turn_x", 0, 1, 1),
    ("place_scales", 2), ("lag1", 0, 0, 2), ("lag1", 0, 0, 3), ("far_edge", 1, 0), ("lag0", 0, 1, 2),
    ("lag1", 0, 1, 0), ("lag1", 0, 1, 1), ("load_x", 1, 1), ("place_scales", 1), ("lag0", 0, 1, 3),
    ("lag2", 0, 1, 0), ("load_words", 1, 2), ("turn_x", 1, 0, 0), ("add_far", "G", 0, 0, 128), ("lag0", 1, 0, 0),
    ("lag0", 1, 0, 1), ("far", 1, 0, 0), ("add_far", "G", 0, 128, 256), ("far", 1, 0, 1), ("turn_x", 1, 0, 1),
    ("lag1", 0, 1, 2), ("lag1", 0, 1, 3), ("lag2", 0, 1, 1), ("lag2", 0, 1, 3), ("lag0", 1, 0, 2),
    ("turn_x", 1, 1, 0), ("lag0", 1, 0, 3), ("lag2", 0, 1, 2), ("far", 1, 0, 2), ("far", 1, 0, 3), ("cast_bias",),
    ("lag1", 1, 0, 0), ("place_scales", 3), ("add_far", "V", 0, 256, 384), ("inter_h", "S", 1, 384, 512),
    ("add_far", "G", 0, 384, 512), ("fix_edge", 0, 1), ("inter_h", "G", 1, 0, 128), ("quant_h", 0, 0),
    ("lag1", 1, 0, 1), ("passes", 0, 0, 0, 0, 512, 0, 1), ("inter_h", "S", 1, 256, 384),
    ("inter_h", "S", 1, 128, 256), ("passes", 0, 0, 1, 0, 512, 0, 1), ("lag1", 1, 0, 2), ("load_words", 2, 3),
    ("far", 1, 1, 0), ("passes", 0, 1, 0, 0, 512, 0, 1), ("lag0", 1, 1, 0), ("passes", 0, 1, 1, 0, 512, 0, 1),
    ("lag1", 1, 0, 3), ("quant_h", 0, 1), ("perm", 4), ("perm", 5), ("load_words", 3, 4), ("perm", 6),
    ("passes", 0, 0, 0, 0, 512, 1, 2), ("add_far", "G", 2, 0, 128), ("lag0", 1, 1, 1),
    ("passes", 0, 0, 1, 0, 512, 1, 2), ("passes", 0, 1, 0, 0, 512, 1, 2), ("far", 1, 1, 1), ("block", 1),
    ("passes", 0, 1, 1, 0, 512, 1, 2), ("turn_x", 1, 1, 1), ("block", 2), ("far", 1, 1, 2), ("perm", 7),
    ("block", 3), ("lag1", 1, 1, 0), ("lag0", 1, 1, 2), ("block", 4), ("lag0", 1, 1, 3), ("lag1", 1, 1, 1),
    ("block", 5), ("turn", 0, 0), ("far", 1, 1, 3), ("lag1", 1, 1, 2), ("turn", 0, 1), ("lag1", 1, 1, 3),
    ("block", 6), ("drain", "S", 0, 0), ("perm", 8), ("drain", "S", 0, 1), ("turn", 0, 2), ("far_edge", 1, 1),
    ("perm", 9), ("turn", 0, 3), ("block", 7), ("add_far", "G", 2, 128, 256), ("add_far", "G", 2, 256, 384),
    ("add_far", "G", 2, 384, 512), ("inter_y", "S", 0, 0, 256), ("block", 8), ("perm", 10), ("drain", "S", 0, 2),
    ("block", 9), ("turn", 1, 0), ("turn", 1, 1), ("drain", "S", 0, 3), ("turn", 1, 2), ("turn", 1, 3),
    ("block", 10), ("perm", 11), ("add_far", "G", 3, 0, 128), ("perm", 12), ("store_y", 0, 0, 2),
    ("inter_y", "S", 0, 256, 512), ("inter_y", "S", 1, 0, 256), ("perm", 13), ("block", 11), ("block", 12),
    ("drain", "S", 1, 0), ("perm", 14), ("add_far", "G", 3, 128, 256), ("block", 13), ("drain", "S", 1, 1),
    ("block", 14), ("turn", 2, 0), ("perm", 15), ("drain", "S", 1, 2), ("store_y", 0, 2, 4),
    ("add_far", "G", 3, 256, 384), ("add_far", "G", 3, 384, 512), ("turn", 2, 1), ("turn", 2, 2), ("quant_h", 1, 0),
    ("quant_h", 1, 1), ("drain", "S", 1, 3), ("turn", 2, 3), ("block", 15), ("inter_y", "S", 1, 256, 512),
    ("block", 16), ("drain", "V", 2, 0), ("drain", "S", 2, 1), ("block", 17), ("block", 18), ("drain", "S", 2, 2),
    ("quant_y", 0, 0, 512), ("drain", "S", 2, 3), ("inter_y", "G", 2, 0, 256), ("block", 19), ("store_y", 1, 0, 2),
    ("turn", 3, 0), ("turn", 3, 1), ("drain", "V", 3, 0), ("turn", 3, 2), ("turn", 3, 3), ("block", 20),
    ("drain", "V", 3, 1), ("inter_y", "V", 2, 256, 512), ("inter_y", "S", 3, 0, 256), ("store_y", 1, 2, 4),
    ("block", 21), ("inter_y", "G", 3, 256, 512), ("store_y", 2, 0, 2), ("quant_y", 1, 0, 512), ("turn", 4, 0),
    ("quant_y", 2, 0, 512), ("turn", 4, 1), ("store_codes", 0, 0, 512), ("quant_y", 3, 0, 512),
    ("drain", "S", 3, 2), ("drain", "S", 3, 3), ("turn", 4, 2), ("inter_y", "G", 4, 0, 256), ("turn", 4, 3),
    ("block", 22), ("inter_y", "S", 4, 256, 512), ("block", 23), ("drain", "V", 4, 0), ("block", 24),
    ("store_y", 2, 2, 4), ("drain", "S", 4, 1), ("store_y", 3, 0, 2), ("store_codes", 1, 0, 512),
    ("store_scales", 0, 0), ("inter_y", "V", 5, 0, 256), ("store_y", 3, 2, 4), ("block", 25), ("drain", "S", 4, 2),
    ("store_codes", 2, 0, 512), ("store_codes", 3, 0, 512), ("turn", 5, 0), ("turn", 5, 1), ("turn", 5, 2),
    ("drain", "S", 4, 3), ("turn", 5, 3), ("store_y", 4, 0, 2), ("inter_y", "G", 5, 256, 512), ("drain", "V", 5, 0),
    ("block", 26), ("drain", "S", 5, 1), ("quant_y", 4, 0, 512), ("drain", "S", 5, 2), ("quant_y", 5, 0, 512),
    ("block", 27), ("block", 28), ("store_y", 4, 2, 4), ("drain", "S", 5, 3), ("turn", 6, 0), ("turn", 6, 1),
    ("store_scales", 0, 1), ("drain", "V", 6, 0), ("store_y", 5, 0, 2), ("drain", "V", 6, 1),
    ("inter_y", "G", 6, 0, 256), ("turn", 6, 2), ("store_scales", 0, 2), ("turn", 6, 3), ("block", 29),
    ("inter_y", "S", 6, 256, 512), ("quant_y", 6, 0, 512), ("block", 30), ("drain", "S", 6, 2),
    ("drain", "V", 6, 3), ("store_codes", 4, 0, 512), ("block", 31), ("turn", 7, 0, 0, 3), ("gate", 7, 3),
    ("value", 7, 3, 0, 128), ("value", 7, 3, 128, 256), ("store_codes", 5, 0, 512), ("turn", 7, 0, 3, 4),
    ("turn", 7, 1, 0, 3), ("store_scales", 0, 3), ("drain", "S", 7, 0), ("store_y", 5, 2, 4),
    ("value", 7, 3, 256, 384), ("turn", 7, 1, 3, 4), ("store_y", 6, 0, 2), ("turn", 7, 2, 0, 3),
    ("store_codes", 6, 0, 512), ("store_scales", 1, 0, 0, 3), ("store_y", 6, 2, 4), ("store_scales", 1, 1, 0, 3),
    ("store_scales", 1, 2, 0, 3), ("inter_y", "V", 7, 0, 256), ("store_scales", 1, 3, 0, 3),
    ("value", 7, 3, 384, 512), ("store_y", 7, 0, 1), ("quant_y", 7, 0, 256), ("turn", 7, 2, 3, 4),
    ("store_codes", 7, 0, 256), ("turn", 7, 3, 0, 3), ("drain", "S", 7, 1), ("store_y", 7, 1, 2),
    ("inter_y", "V", 7, 256, 512), ("quant_y", 7, 256, 512), ("drain", "S", 7, 2), ("turn", 7, 3, 3, 4),
    ("drain", "S", 7, 3), ("store_y", 7, 2, 3), ("store_scales", 1, 0, 3, 4), ("store_scales", 1, 1, 3, 4),
    ("store_scales", 1, 2, 3, 4), ("store_y", 7, 3, 4), ("store_scales", 1, 3, 3, 4), ("store_codes", 7, 256, 512),
]


def tile_lag_mix_gated_channels_g4_kernel(
    tc, x, taps, wv_words, wv_scales, wg_words, wg_scales, bv, bg, out_0, out_1, out_2
):
    nc = tc.nc
    w_words = (wg_words, wv_words)
    w_scales = (wg_scales, wv_scales)
    y_rows = out_0.rearrange("b u n -> (b u) n")

    with ExitStack() as ctx:
        keep = ctx.enter_context(tc.tile_pool(name="keep", bufs=1))
        psum = ctx.enter_context(tc.psum_pool(name="psum", bufs=1))
        ctx.enter_context(tc.manual_schedule())

        banks = [psum.tile([P, 512], F32, name="bank%d" % i) for i in range(8)]
        ident = keep.tile([P, P], F32, name="ident")
        warm = keep.tile([P, 1], F32, name="warm")
        warm_out = keep.tile([P, 1], F32, name="warm_out")
        taps_raw = keep.tile([P, 6, 4], BF16, name="taps_raw")
        taps_f = keep.tile([P, 3, 8], F32, name="taps_f")
        bias_raw = [keep.tile([P, 4, 4], BF16, name="bias_raw%d" % m) for m in range(2)]
        bias_f = keep.tile([P, 2, 16], F32, name="bias_f")
        x_sb = [[keep.tile([P, 2, 2, 512], BF16, name="x%d%d" % (h, g)) for g in range(2)] for h in range(2)]
        hist = keep.tile([P, C], BF16, name="hist")
        hist_w = keep.tile([P, 4, 16], F32, name="hist_w")
        edge1 = keep.tile([P, 8, 16], F32, name="edge1")
        edge = keep.tile([P, 8, 16], F32, name="edge")
        w_raw = keep.tile([P, 4, 4096], U8, name="w_raw", align_bytes=64)
        s_raw = keep.tile([P, N], U8, name="s_raw")
        s_mid = keep.tile([P, N], U8, name="s_mid")
        w_perm = keep.tile([P, max(16 - 4 * KB, 1), 4, 256], U8, align_bytes=64, name="w_perm")
        s_perm = keep.tile([P, 4, N], U8, align_bytes=64, name="s_perm")
        h_codes = keep.tile([P, 2, 2, TOK], U32, align_bytes=64, name="h_codes")
        h_scales = keep.tile([P, 2, 2, TOK], U8, align_bytes=64, name="h_scales")
        y_scales = keep.tile([P, 2, 4, TOK], U8, align_bytes=64, name="y_scales")
        accs = [keep.tile([P, 4, 2, T], F32, name="acc%d" % i) for i in range(NA)]
        fars = [keep.tile([P, 4, 2, T], F32, name="far%d" % i) for i in range(NF)]
        rows = keep.tile([P, 4, 2, T], BF16, name="rows")
        inters = [keep.tile([P, TOK, 4], BF16, name="inter%d" % i, align_bytes=64) for i in range(2)]
        ys = [keep.tile([P, 4, TOK], F32, name="y%d" % i) for i in range(NY)]
        gates = [keep.tile([P, TOK], F32, name="gate%d" % i) for i in range(3)]
        outs = [keep.tile([P, 4, 512], F32, name="o%d" % i) for i in range(NO)]
        ybfs = [keep.tile([P, TOK, 4], BF16, name="ybf%d" % i, align_bytes=64) for i in range(NB)]
        codes = [keep.tile([P, TOK], U32, name="codes%d" % i, align_bytes=64) for i in range(3)]
        eng = {"V": nc.vector, "S": nc.scalar, "G": nc.gpsimd}

        def load_x(h, g):
            for b in range(2):
                nc.sync.dma_start(
                    out=x_sb[h][g][:, b, :, :],
                    in_=x[2 * h + b, PAST:, 512 * g : 512 * (g + 1)].rearrange("(a p) c -> p a c", p=P),
                )

        def load_words(j0, j1):
            cols = slice(1024 * j0, 1024 * j1)
            for m in range(2):
                nc.sync.dma_start(
                    out=w_raw[:, 2 * m : 2 * m + 2, cols].bitcast(I32),
                    in_=w_words[m].rearrange("g p w -> p g w")[:, :, cols].bitcast(I32),
                )

        def load_scales():
            for m in range(2):
                nc.sync.dma_start(out=s_raw[32 * m : 32 * (m + 1), :].bitcast(I32),
                                  in_=w_scales[m].rearrange("g q n -> (g q) n").bitcast(I32))

        def place_scales(i):
            for q in range(4):
                nc.sync.dma_start(
                    out=s_perm[32 * q : 32 * q + 4, i, :].bitcast(I32),
                    in_=s_mid[16 * i + 4 * q : 16 * i + 4 * q + 4, :].bitcast(I32),
                )

        def setup():
            make_identity(nc, ident[:])
            nc.vector.memset(s_raw[64:128, :].bitcast(I32), 0)
            nc.vector.memset(hist[:].bitcast(I32), 0)
            nc.vector.memset(warm[:], 0.0)
            nc.scalar.dma_start(out=taps_raw[:], in_=taps.rearrange("j (g p t) -> p (j g) t", p=P, t=4))
            nc.scalar.dma_start(out=hist[0:16, :], in_=x[:, 0:PAST, :])
            nc.scalar.activation(out=warm_out[:], in_=warm[:], func=ACT.Sigmoid)

        def clear_planes():
            nc.vector.memset(s_perm[:].rearrange("p i n -> p (i n)").bitcast(I32), 0)

        def load_bias():
            for m, vec in enumerate((bg, bv)):
                nc.sync.dma_start(out=bias_raw[m][:], in_=vec.rearrange("(j p t) -> p j t", p=P, t=4))

        def cast_taps():
            nc.vector.tensor_copy(out=taps_f[:].rearrange("p j k -> p (j k)"), in_=taps_raw[:].rearrange("p a t -> p (a t)"))

        def cast_bias():
            for m in range(2):
                nc.scalar.copy(out=bias_f[:, m, :], in_=bias_raw[m][:].rearrange("p j t -> p (j t)"))

        def perm_scales():
            w = 512 * KB
            if KB:
                nc.vector.tensor_copy(out=s_mid[:, :w].bitcast(I32), in_=s_raw[:, :w].bitcast(I32))
            if KB < 4:
                nc.vector.tensor_copy(
                    out=s_mid[:, w:].rearrange("p (j t c) -> p j t c", c=P, t=4),
                    in_=s_raw[:, w:].rearrange("p (j c t) -> p j t c", c=P, t=4))

        x_bank = {(0, 0): 0, (0, 1): 2, (1, 0): 6, (1, 1): 4}
        acc_of = {(h, g): accs[(2 * h + g) % NA] for h in range(2) for g in range(2)}
        far_of = {(0, 0): fars[0], (1, 0): fars[1], (1, 1): fars[0]}

        def turn_x(h, g, u):
            words = x_sb[h][g][:].bitcast(F32)
            for b in range(2):
                for a in range(2):
                    k = 2 * b + a
                    nc.tensor.transpose(banks[x_bank[h, g] + u][:, P * k : P * (k + 1)], words[:, b, a, u:256:2], ident[:])

        def turn_hist():
            hist_words = hist[:].bitcast(F32)
            for gu in range(4):
                g, u = divmod(gu, 2)
                nc.tensor.transpose(banks[4][:, P * gu : P * (gu + 1)], hist_words[:, 256 * g + u : 256 * (g + 1) : 2], ident[:])

        def copy_hist():
            nc.scalar.copy(out=hist_w[:], in_=banks[4][:].rearrange("p (k r) -> p k r", k=4)[:, :, 0:16])

        def make_edge():
            hist_b = hist_w[:].rearrange("p k r -> p (k r)").bitcast(BF16).rearrange("p (k n e) -> p k e n", k=4, e=2)
            for dst, j in ((edge, 2), (edge1, 1)):
                nc.gpsimd.tensor_tensor(
                    out=dst[:].rearrange("p (k e) n -> p k e n", e=2), in0=hist_b,
                    in1=taps_f[:, j, :].rearrange("p (k e) -> p k e", e=2).unsqueeze(3).to_broadcast([P, 4, 2, 16]),
                    op=ALU.mult)
            ev = edge[:].rearrange("p k (b r) -> p (k b) r", r=4)
            e1v = edge1[:].rearrange("p k (b r) -> p (k b) r", r=4)
            nc.gpsimd.tensor_tensor(out=ev[:, :, 0:2], in0=ev[:, :, 0:2], in1=e1v[:, :, 2:4], op=ALU.add)

        def frames(h, g, t):
            u, e = divmod(t, 2)
            return banks[x_bank[h, g] + u][:].bitcast(BF16).rearrange("p (b r e) -> p b r e", b=2, e=2)[:, :, :, e]

        def tap(j, g, t):
            return taps_f[:, j, 4 * g + t : 4 * g + t + 1]

        def edge_of(h, g):
            return edge[:, 4 * g : 4 * g + 4, 8 * h : 8 * h + 8].rearrange("p t (b r) -> p t b r", b=2)

        def lag0(h, g, t):
            nc.scalar.activation(out=acc_of[h, g][:, t, :, :], in_=frames(h, g, t), func=ACT.Copy, scale=tap(0, g, t))

        def lag1(h, g, t):
            acc = acc_of[h, g]
            nc.vector.scalar_tensor_tensor(
                out=acc[:, t, :, 2:], in0=frames(h, g, t)[:, :, : T - 2], scalar=tap(1, g, t),
                in1=acc[:, t, :, 2:], op0=ALU.mult, op1=ALU.add)

        def lag2(h, g, t):
            nc.vector.scalar_tensor_tensor(
                out=rows[:, t, :, 4:], in0=frames(h, g, t)[:, :, : T - 4], scalar=tap(2, g, t),
                in1=acc_of[h, g][:, t, :, 4:], op0=ALU.mult, op1=ALU.add)

        def fix_edge(h, g):
            nc.vector.tensor_tensor(out=rows[:, :, :, 0:4], in0=acc_of[h, g][:, :, :, 0:4], in1=edge_of(h, g), op=ALU.add)

        def inter_h(e, g, c0, c1):
            interleave(e, inters[g], rows[:].rearrange("p t b u -> p t (b u)"), c0, c1)

        def far(h, g, t):
            nc.scalar.activation(out=far_of[h, g][:, t, :, 4:], in_=frames(h, g, t)[:, :, : T - 4], func=ACT.Copy,
                                 scale=tap(2, g, t))

        def far_edge(h, g):
            nc.scalar.copy(out=far_of[h, g][:, :, :, 0:4], in_=edge_of(h, g))

        def add_far(e, hg, c0, c1):
            h, g = divmod(hg, 2)
            terms = [a[:].rearrange("p t b u -> p t (b u)")[:, :, c0:c1].rearrange("p t (c i) -> p c t i", i=2)
                     for a in (acc_of[h, g], far_of[h, g])]
            eng[e].tensor_tensor(out=inters[g][:, c0:c1, :].rearrange("p (c i) t -> p c t i", i=2),
                                 in0=terms[0], in1=terms[1], op=ALU.add)

        def interleave(e, dst, src, c0, c1):
            run = 2 if e == "G" else 4
            o = dst[:, c0:c1, :].rearrange("p (c i) t -> p c t i", i=run)
            s = src[:, :, c0:c1].rearrange("p t (c i) -> p c t i", i=run)
            if e == "S":
                nc.scalar.copy(out=o, in_=s)
            elif e == "G":
                nc.gpsimd.tensor_scalar(out=o, in0=s, scalar1=1.0, scalar2=-0.0, op0=ALU.mult, op1=ALU.add)
            else:
                nc.vector.tensor_copy(out=o, in_=s)

        def quant_h(h, g):
            nc.vector.quantize_mx(out=h_codes[:, h, g, :].bitcast(FP8X4), scales=h_scales[:, h, g, :],
                                  in_=inters[g][:].rearrange("p n t -> p (n t)"))

        def perm(k):
            j, t = divmod(k, 4)
            nc.vector.tensor_copy(
                out=w_perm[:, k - 4 * KB, :, :].rearrange("p i (c e) -> p i c e", e=2),
                in_=w_raw[:, :, 1024 * j : 1024 * (j + 1)].rearrange("p i (c t e) -> p i c t e", t=4, e=2)[:, :, :, t, :])

        def stationary(j, t, i):
            if j < KB:
                return w_raw[:, i, 1024 * j + 256 * t : 1024 * j + 256 * (t + 1)]
            return w_perm[:, 4 * (j - KB) + t, i, :]

        def bias(m, n, t):
            j = UNITS[n][1]
            return bias_f[:, m, 4 * j + t : 4 * j + t + 1]

        def slot(n, t, c0):
            return 4 * n + t + (4 if HALF and n == 7 and c0 >= 256 else 0)

        def passes(n, t, m, c0, c1, g0=0, g1=2):
            h, j = UNITS[n]
            acc = banks[(2 * slot(n, t, c0) + m) % 4]
            for g in range(g0, g1):
                i = 2 * m + g
                nc.tensor.matmul_mx(
                    out=acc[:, c0:c1], lhsT=stationary(j, t, i).bitcast(FP4X4),
                    lhsT_scale=s_perm[:, i, 512 * j + P * t : 512 * j + P * (t + 1)],
                    rhs=h_codes[:, h, g, c0:c1].bitcast(FP8X4), rhs_scale=h_scales[:, h, g, c0:c1],
                    start=(g == 0), stop=(g == 1))

        def mx(n, t, c0=0, c1=TOK, w=TOK):
            for m in range(2):
                for c in range(c0, c1, w):
                    passes(n, t, m, c, c + w)

        def gate(n, t, c0=0, c1=TOK):
            nc.scalar.activation(out=gates[slot(n, t, c0) % 3][:, c0:c1], in_=banks[2 * slot(n, t, c0) % 4][:, c0:c1],
                                 func=ACT.Sigmoid, bias=bias(0, n, t))

        def value(n, t, c0=0, c1=TOK):
            nc.vector.scalar_tensor_tensor(
                out=ys[n % NY][:, t, c0:c1], in0=banks[(2 * slot(n, t, c0) + 1) % 4][:, c0:c1], scalar=bias(1, n, t),
                in1=gates[slot(n, t, c0) % 3][:, c0:c1], op0=ALU.add, op1=ALU.mult)

        def block(s):
            if s < 32 and s > 1:
                mx(*divmod(s, 4))
            if 0 <= s - SKEW < 31:
                gate(*divmod(s - SKEW, 4))
                value(*divmod(s - SKEW, 4))

        uses = []
        for n in range(8):
            uses.extend([("turn", n, k) for k in range(4)])
            if UNITS[n][1] < KB:
                uses.extend([("back", n, k) for k in range(2)])

        def ring(kind, n, k):
            i = uses.index((kind, n, k))
            return banks[6 + i % 2] if i < EARLY else banks[4 + (i - EARLY) % 4]

        def turn_bank(n, k):
            return ring("turn", n, k)

        def turn(n, k, t0=0, t1=4):
            for t in range(t0, t1):
                nc.tensor.transpose(turn_bank(n, k)[:, P * t : P * (t + 1)], ys[n % NY][:, t, P * k : P * (k + 1)], ident[:])

        def drain(e, n, k):
            o = outs[n % NO][:, k, :]
            s = turn_bank(n, k)[:]
            if UNITS[n][1] >= KB:
                o = o.rearrange("p (c t) -> p c t", t=4)
                s = s.rearrange("p (t c) -> p c t", t=4)
            if e == "S":
                nc.scalar.copy(out=o, in_=s)
            else:
                nc.vector.tensor_copy(out=o, in_=s)

        def store_y(n, k0, k1):
            h, j = UNITS[n]
            nc.sync.dma_start(
                out=y_rows[TOK * h + P * k0 : TOK * h + P * k1, 512 * j : 512 * (j + 1)].rearrange("(k p) n -> p k n", p=P),
                in_=outs[n % NO][:, k0:k1, :])

        def inter_y(e, n, c0, c1):
            interleave(e, ybfs[n % NB], ys[n % NY][:], c0, c1)

        def quant_y(n, c0, c1):
            h, j = UNITS[n]
            nc.vector.quantize_mx(out=codes[n % 3][:, c0:c1].bitcast(FP8X4), scales=y_scales[:, h, j, c0:c1],
                                  in_=ybfs[n % NB][:, c0:c1, :].rearrange("p n t -> p (n t)"))

        def store_codes(n, c0, c1):
            h, j = UNITS[n]
            nc.sync.dma_start(
                out=out_1[j, :, TOK * h + c0 : TOK * h + c1, :].rearrange("p n t -> p (n t)").bitcast(I32),
                in_=codes[n % 3][:, c0:c1].bitcast(I32))

        def store_scales(h, q, j0=0, j1=4):
            nc.sync.dma_start(
                out=out_2[j0:j1, 4 * q : 4 * q + 4, TOK * h : TOK * (h + 1)].rearrange("j r n -> r j n").bitcast(I32),
                in_=y_scales[32 * q : 32 * q + 4, h, j0:j1, :].bitcast(I32))

        steps = dict(
            setup=setup, lag2=lag2, fix_edge=fix_edge, inter_h=inter_h, clear_planes=clear_planes, block=block,  load_bias=load_bias, load_x=load_x, load_words=load_words, load_scales=load_scales, place_scales=place_scales,
            cast_taps=cast_taps, cast_bias=cast_bias, perm_scales=perm_scales, turn_x=turn_x, turn_hist=turn_hist,
            copy_hist=copy_hist, make_edge=make_edge, lag0=lag0, lag1=lag1, far=far, far_edge=far_edge, add_far=add_far,
            quant_h=quant_h, perm=perm, passes=passes, mx=mx,
            gate=gate, value=value, turn=turn, drain=drain, store_y=store_y, inter_y=inter_y, quant_y=quant_y,
            store_codes=store_codes, store_scales=store_scales)
        for step in PLAN:
            steps[step[0]](*step[1:])
